import numpy as np
import ml_dtypes


def mxq(x, axis, fmt="e4m3"):
    dtype, down = {"e4m3": (ml_dtypes.float8_e4m3fn, 7), "e5m2": (ml_dtypes.float8_e5m2, 14)}[fmt]
    v = np.moveaxis(np.asarray(x, np.float32).astype(ml_dtypes.bfloat16).astype(np.float64), axis, -1)
    blocks = v.reshape(v.shape[:-1] + (-1, 32))
    amax = np.abs(blocks).max(-1, keepdims=True)
    byte = np.maximum(np.where(amax > 0, np.frexp(amax)[1] - 1 + 127, 0) - down, 1)
    scale = np.exp2(byte - 127.0)
    codes = (blocks / scale).astype(np.float32).astype(dtype).astype(np.float64)
    return np.moveaxis((codes * scale).reshape(v.shape), -1, axis)


WIDE = False


def mx_kscale(k):
    if not WIDE:
        return np.ones(k)
    levels = np.array([10, -10, 5, -5, 0])
    if k % 512:
        return np.exp2(np.random.permutation(np.resize(levels, k // 32))).repeat(32)
    a = np.empty((k // 512, 16))
    for p in range(k // 512):
        a[p, :8] = np.random.permutation(np.resize(levels, 8))
        for g in range(8):
            far = levels[np.abs(levels - a[p, g]) >= 10]
            a[p, g + 8] = far[np.random.randint(len(far))]
    return np.exp2(a.ravel()).repeat(32)


def f64(x):
    return np.asarray(x).astype(np.float64)


def striped(idx):
    return np.tile(idx.reshape(-1, 16).T, (8, 1)).astype(np.uint16)


def unstriped(offs):
    return offs[:16].T.reshape(-1).astype(np.int64)


def striped8(idx):
    return np.concatenate([x.reshape(-1, 16).T for x in idx]).astype(np.uint16)


def runs(offs, k):
    lists = np.stack([offs[16 * r : 16 * r + 16].T.reshape(-1) for r in range(8)]).astype(np.int64)
    return lists[np.arange(k) % 512 // 64]


def pack_weight(w):
    k, n = w.shape
    w = f64(np.asarray(w, np.float32).astype(ml_dtypes.bfloat16)).reshape(k // 32, 32, n)
    amax = np.abs(w).max(1)
    byte = np.clip(np.where(amax > 0, np.frexp(amax)[1] - 1 + 127 - 7, 1), 1, 254)
    scaled = (w * np.exp2(127.0 - byte)[:, None, :]).reshape(k, n).astype(np.float32)
    words = np.ascontiguousarray(scaled.reshape(k // 512, 128, 4, n).transpose(0, 1, 3, 2)).astype(ml_dtypes.float8_e4m3fn).view(np.uint8)
    return words, np.ascontiguousarray(byte.astype(np.uint8).reshape(k // 512, 16, n))


def unpack_weight(words, scales):
    g, p, n, _ = words.shape
    vals = np.ascontiguousarray(words).view(ml_dtypes.float8_e4m3fn).astype(np.float64) * np.repeat(np.exp2(scales.astype(np.float64) - 127.0), 8, axis=1)[..., None]
    return vals.transpose(0, 1, 3, 2).reshape(g * 512, n)


E2M1 = np.array([0.0, 0.5, 1.0, 1.5, 2.0, 3.0, 4.0, 6.0, -0.0, -0.5, -1.0, -1.5, -2.0, -3.0, -4.0, -6.0])


def pack_fp4(w):
    k, n = w.shape
    w = f64(np.asarray(w, np.float32).astype(ml_dtypes.bfloat16)).reshape(k // 32, 32, n)
    amax = np.abs(w).max(1)
    mant, ex = np.frexp(amax / 6.0)
    byte = np.clip(np.where(amax > 0, np.where(mant > 0.5, ex, ex - 1) + 127, 1), 1, 254)
    scaled = (w * np.exp2(127.0 - byte)[:, None, :]).reshape(k, n).astype(np.float32)
    c = np.ascontiguousarray(scaled.reshape(k // 512, 128, 4, n).transpose(0, 1, 3, 2)).astype(ml_dtypes.float4_e2m1fn).view(np.uint8) & 0xF
    words = (c[..., 0::2] | (c[..., 1::2] << 4)).reshape(k // 512, 128, 2 * n)
    return np.ascontiguousarray(words), np.ascontiguousarray(byte.astype(np.uint8).reshape(k // 512, 16, n))


def unpack_fp4(words, scales):
    g, _, n = scales.shape
    words = np.ascontiguousarray(words).reshape(g, 128, n, 2)
    nib = np.empty((g, 128, n, 4), np.uint8)
    nib[..., 0::2] = words & 0xF
    nib[..., 1::2] = words >> 4
    vals = E2M1[nib] * np.repeat(np.exp2(scales.astype(np.float64) - 127.0), 8, axis=1)[..., None]
    return vals.transpose(0, 1, 3, 2).reshape(g * 512, n)


def sigmoid(v):
    return 1.0 / (1.0 + np.exp(-np.maximum(v, -700.0)))

def planes(y):
    n, m = y.shape
    v = y.astype(np.float32).astype(ml_dtypes.bfloat16).astype(np.float64).reshape(n // 32, 32, m)
    top = np.abs(v).max(1)
    byte = np.clip(np.where(top > 0, np.frexp(top)[1] - 1 + 127 - 7, 1), 1, 254)
    codes = (v * np.exp2(127.0 - byte)[:, None, :]).reshape(n, m).astype(np.float32).astype(ml_dtypes.float8_e4m3fn).view(np.uint8)
    words = codes.reshape(n // 512, 128, 4, m).transpose(0, 1, 3, 2)
    return np.ascontiguousarray(words), np.ascontiguousarray(byte.astype(np.uint8).reshape(n // 512, 16, m))


K, T, S, H, G = 512, 2048, 512, 512, 2048


def setup_inputs():
    n = np.random.standard_normal
    s = mx_kscale(K)[:, None]
    packed_xT = pack_weight(n((K, T)) * s)
    packed_w1 = pack_fp4(n((K, H)) / np.sqrt(K) / s)
    packed_dT = pack_weight(n((K, G)) / s)
    return {
        "x_words": packed_xT[0],
        "x_scales": packed_xT[1],
        "w1_words": packed_w1[0],
        "w1_scales": packed_w1[1],
        "gs": (np.random.uniform(0.5, 1.5, (K, 1)) * s).astype(np.float32),
        "d_words": packed_dT[0],
        "d_scales": packed_dT[1],
        "offs": striped(np.random.permutation(T)[:S]),
        "n1": striped8(np.stack([np.random.permutation(S) for _ in range(8)])),
        "n2": striped8(np.stack([np.random.permutation(S) for _ in range(8)])),
        "n3": striped8(np.stack([np.random.permutation(S) for _ in range(8)])),
        "k1": striped8(np.random.randint(0, G, (8, H))),
        "n4": striped8(np.stack([np.random.permutation(S) for _ in range(8)])),
        "n5": striped8(np.stack([np.random.permutation(S) for _ in range(8)])),
    }


def reference(x_words, x_scales, w1_words, w1_scales, gs, d_words, d_scales, offs, n1, n2, n3, k1, n4, n5):
    d_k1 = unpack_weight(d_words, d_scales)[np.arange(K)[:, None], runs(k1, K)]
    xq = unpack_weight(x_words, x_scales)[:, unstriped(offs)]
    y = unpack_fp4(w1_words, w1_scales).T @ xq
    z = f64(gs) * (0.75 * (y * (y[np.arange(H)[:, None], runs(n1, H)]) + (y[np.arange(H)[:, None], runs(n2, H)]) * (y[np.arange(H)[:, None], runs(n3, H)])))
    h = 0.0625 * ((d_k1.T @ mxq(z, 0, "e4m3")))
    st = h * (sigmoid(h[np.arange(H)[:, None], runs(n4, H)]))
    out_0 = st - (st[np.arange(H)[:, None], runs(n5, H)])
    return (out_0,) + planes(out_0)

@@ -1,0 +1,206 @@
+from contextlib import ExitStack
+
+import concourse.mybir as mybir
+
+F32 = mybir.dt.float32
+BF16 = mybir.dt.bfloat16
+I32 = mybir.dt.int32
+U32 = mybir.dt.uint32
+U16 = mybir.dt.uint16
+U8 = mybir.dt.uint8
+FP8X4 = mybir.dt.float8_e4m3fn_x4
+FP4X4 = mybir.dt.float4_e2m1fn_x4
+ALU = mybir.AluOpType
+ACT = mybir.ActivationFunctionType
+
+P = 128
+PACK = 4
+S = 512
+T = 2048
+PIECES = ((0, 256), (256, 128), (384, 128))
+HALVES = ((0, 256), (256, 256))
+
+FLOPS = 2 * 2 * 512 * 512 * 512
+
+
+def tile_picked_densedothopg_none_po_kernel(
+    tc, x_words, x_scales, w1_words, w1_scales, gs, d_words, d_scales, offs, n1, n2, n3, k1, n4, n5, out_0, out_1, out_2
+):
+    nc = tc.nc
+    with ExitStack() as ctx:
+        keep = ctx.enter_context(tc.tile_pool(name="keep", bufs=1))
+        psum = ctx.enter_context(tc.psum_pool(name="psum", bufs=1))
+
+        def tile(shape, dtype, name):
+            return keep.tile(shape, dtype, name=name, align_bytes=64)
+
+        def load_list(src, name):
+            lst = tile([P, S // 16], U16, name)
+            nc.sync.dma_start(lst[:], src)
+            return lst
+
+        def entries(lst, c0, w):
+            return lst[:, c0 // 16 : (c0 + w) // 16]
+
+        xs_win = tile([P, T], U8, "xs_win")
+        w1s_raw = tile([P, S], U8, "w1s_raw")
+        ds_win = tile([P, T], U8, "ds_win")
+        ds_mx = tile([P, S], U8, "ds_mx")
+        nc.gpsimd.memset(w1s_raw[:].bitcast(I32), 0)
+        nc.vector.memset(xs_win[:].bitcast(I32), 0)
+        warm = tile([P, 2], F32, "warm")
+        nc.vector.memset(warm[:, 0:1], 0.0)
+        nc.vector.memset(ds_win[:].bitcast(I32), 0)
+        nc.vector.memset(ds_mx[:].bitcast(I32), 0)
+
+        offs_t = load_list(offs, "offs_t")
+        xw_win = tile([P, T], I32, "xw_win")
+        nc.sync.dma_start(xw_win[:], x_words[0].rearrange("p n t -> p (n t)").bitcast(I32))
+        w1w_raw = tile([P, 2 * S], U8, "w1w_raw")
+        nc.scalar.dma_start(w1w_raw[:].bitcast(I32), w1_words[0].bitcast(I32))
+        for q in range(4):
+            nc.scalar.dma_start(xs_win[32 * q : 32 * q + 4, :].bitcast(I32), x_scales[0, 4 * q : 4 * q + 4, :].bitcast(I32))
+        for q in range(4):
+            eng = nc.gpsimd if q < 2 else nc.scalar
+            eng.dma_start(w1s_raw[32 * q : 32 * q + 4, :].bitcast(I32), w1_scales[0, 4 * q : 4 * q + 4, :].bitcast(I32))
+        nc.scalar.activation(warm[:, 1:2], warm[:, 0:1], ACT.Sigmoid)
+        gs_raw = tile([P, PACK], F32, "gs_raw")
+        nc.gpsimd.dma_start(gs_raw[:], gs.rearrange("(p t) o -> p (t o)", t=PACK))
+        nc.gpsimd.dma_start(ds_win[0:P:8, :].bitcast(I32), d_scales[0].bitcast(I32))
+        n2_t = load_list(n2, "n2_t")
+        k1_t = load_list(k1, "k1_t")
+        n1_t = load_list(n1, "n1_t")
+        n3_t = load_list(n3, "n3_t")
+        dw_win = tile([P, T], I32, "dw_win")
+        nc.sync.dma_start(dw_win[:], d_words[0].rearrange("p n t -> p (n t)").bitcast(I32))
+        n4_t = load_list(n4, "n4_t")
+        n5_t = load_list(n5, "n5_t")
+
+        xs = tile([P, S], U8, "xs")
+        nc.vector.tensor_copy(xs[:], xs_win[:].indirect(offs_t[:]))
+        w1w = tile([P, 2 * S], U8, "w1w")
+        nc.vector.tensor_copy(
+            w1w[:].rearrange("p (t m b) -> p t m b", t=PACK, b=2), w1w_raw[:].rearrange("p (m t b) -> p t m b", t=PACK, b=2)
+        )
+        w1s = tile([P, S], U8, "w1s")
+        nc.vector.tensor_copy(w1s[:].rearrange("p (t m) -> p t m", t=PACK), w1s_raw[:].rearrange("p (m t) -> p t m", t=PACK))
+        xw = tile([P, S], U32, "xw")
+        nc.vector.tensor_copy(xw[:], xw_win[:].bitcast(U32).indirect(offs_t[:]))
+        gain = tile([P, PACK], F32, "gain")
+        nc.vector.tensor_scalar(gain[:], gs_raw[:], 0.75, None, ALU.mult)
+
+        y, yg = [], []
+        for t in range(PACK):
+            acc = psum.tile([P, S], F32, name=f"y_acc{t}")
+            nc.tensor.matmul_mx(
+                out=acc[:],
+                lhsT=w1w[:, 2 * P * t : 2 * P * (t + 1)].bitcast(FP4X4),
+                lhsT_scale=w1s[:, P * t : P * (t + 1)],
+                rhs=xw[:].bitcast(FP8X4),
+                rhs_scale=xs[:],
+                start=True,
+                stop=True,
+            )
+            y.append(tile([P, S], F32, f"y{t}"))
+            yg.append(tile([P, S], F32, f"yg{t}"))
+            nc.scalar.copy(y[t][:], acc[:])
+            nc.scalar.activation(yg[t][:], acc[:], ACT.Copy, scale=gain[:, t : t + 1])
+
+        ds_g = tile([P, S], U8, "ds_g")
+        nc.vector.tensor_copy(ds_g[:], ds_win[:].indirect(k1_t[:]))
+        ds_d = tile([P, S], U8, "ds_d")
+        nc.vector.tensor_copy(ds_d[:].rearrange("p (t m) -> p t m", t=PACK), ds_g[:].rearrange("p (m t) -> p t m", t=PACK))
+        for r in range(4):
+            nc.sync.dma_start(ds_mx[r:P:32, :].bitcast(I32), ds_d[8 * r : P : 32, :].bitcast(I32))
+
+        h_acc = [psum.tile([P, S], F32, name=f"h_acc{t}") for t in range(PACK)]
+        h = [tile([P, S], F32, f"h{t}") for t in range(PACK)]
+        sig0 = tile([P, S], F32, "sig0")
+        dw = tile([P, S], U32, "dw")
+        for c, (c0, w) in enumerate(PIECES):
+            cols = slice(c0, c0 + w)
+            g2 = tile([P, PACK, w], F32, f"g2_{c}")
+            pa = tile([P, PACK, w], F32, f"pa_{c}")
+            pb = tile([P, PACK, w], F32, f"pb_{c}")
+            for t in range(PACK):
+                nc.vector.tensor_copy(g2[:, t, :], y[t][:].indirect(entries(n2_t, c0, w)))
+                nc.vector.tensor_tensor(pa[:, t, :], y[t][:].indirect(entries(n1_t, c0, w)), yg[t][:, cols], ALU.mult)
+                nc.vector.tensor_tensor(pb[:, t, :], yg[t][:].indirect(entries(n3_t, c0, w)), g2[:, t, :], ALU.mult)
+            if c == 0:
+                dw_g = tile([P, S], U32, "dw_g")
+                nc.vector.tensor_copy(dw_g[:], dw_win[:].bitcast(U32).indirect(k1_t[:]))
+            zb = tile([P, PACK * w], BF16, f"zb_{c}")
+            nc.vector.tensor_tensor(
+                zb[:].rearrange("p (c i t) -> p c t i", i=2, t=PACK),
+                pa[:].rearrange("p t (c i) -> p c t i", i=2),
+                pb[:].rearrange("p t (c i) -> p c t i", i=2),
+                ALU.add,
+            )
+            if c == 0:
+                nc.vector.tensor_copy(dw[:].rearrange("p (t m) -> p t m", t=PACK), dw_g[:].rearrange("p (m t) -> p t m", t=PACK))
+            zw = tile([P, w], U32, f"zw_{c}")
+            zs = tile([P, w], U8, f"zs_{c}")
+            nc.vector.quantize_mx(out=zw[:].bitcast(FP8X4), scales=zs[:], in_=zb[:])
+            for t in range(PACK):
+                nc.tensor.matmul_mx(
+                    out=h_acc[t][:, cols],
+                    lhsT=dw[:, P * t : P * (t + 1)].bitcast(FP8X4),
+                    lhsT_scale=ds_mx[:, P * t : P * (t + 1)],
+                    rhs=zw[:].bitcast(FP8X4),
+                    rhs_scale=zs[:],
+                    start=True,
+                    stop=True,
+                )
+            nc.scalar.activation(sig0[:, cols], h_acc[0][:, cols], ACT.Sigmoid, scale=0.0625)
+            for t in range(PACK):
+                nc.scalar.activation(h[t][:, cols], h_acc[t][:, cols], ACT.Copy, scale=0.0625)
+
+        st = [tile([P, S], F32, f"st{t}") for t in range(PACK)]
+        nst = [tile([P, S], F32, f"nst{t}") for t in range(PACK)]
+        res = [tile([P, PACK, w], F32, f"res_{c}") for c, (c0, w) in enumerate(PIECES)]
+
+        def difference(c, t):
+            c0, w = PIECES[c]
+            nc.vector.tensor_tensor(res[c][:, t, :], nst[t][:].indirect(entries(n5_t, c0, w)), st[t][:, c0 : c0 + w], ALU.add)
+
+        for t in range(PACK):
+            if t == 0:
+                for c0, w in HALVES:
+                    nc.vector.tensor_tensor(
+                        st[0][:, c0 : c0 + w], sig0[:].indirect(entries(n4_t, c0, w)), h[0][:, c0 : c0 + w], ALU.mult
+                    )
+            else:
+                sg = tile([P, S], F32, f"sg{t}")
+                for c0, w in HALVES:
+                    nc.scalar.activation(sg[:, c0 : c0 + w], h[t][:].indirect(entries(n4_t, c0, w)), ACT.Sigmoid)
+                nc.vector.tensor_tensor(st[t][:], sg[:], h[t][:], ALU.mult)
+            if t < 2:
+                nc.vector.tensor_scalar(nst[t][:], st[t][:], -1.0, None, ALU.mult)
+            else:
+                nc.scalar.activation(nst[t][:], st[t][:], ACT.Copy, scale=-1.0)
+            if t > 0:
+                difference(0, t - 1)
+        difference(0, PACK - 1)
+
+        out_rows = out_0.rearrange("(p t) s -> p t s", t=PACK)
+        out_words = out_1[0].rearrange("p n t -> p (n t)").bitcast(I32)
+        os_ = tile([P, S], U8, "os")
+        for c, (c0, w) in enumerate(PIECES):
+            cols = slice(c0, c0 + w)
+            if c > 0:
+                for t in range(PACK):
+                    difference(c, t)
+            nc.sync.dma_start(out_rows[:, :, cols], res[c][:])
+            ob = tile([P, PACK * w], BF16, f"ob_{c}")
+            dst = ob[:].rearrange("p (c i t) -> p c t i", i=2, t=PACK)
+            srcv = res[c][:].rearrange("p t (c i) -> p c t i", i=2)
+            if c < len(PIECES) - 1:
+                nc.scalar.copy(dst, srcv)
+            else:
+                nc.vector.tensor_copy(dst, srcv)
+            ow = tile([P, w], U32, f"ow_{c}")
+            nc.vector.quantize_mx(out=ow[:].bitcast(FP8X4), scales=os_[:, cols], in_=ob[:])
+            nc.scalar.dma_start(out_words[:, cols], ow[:].bitcast(I32))
+        for q in range(4):
+            eng = nc.sync if q % 2 == 0 else nc.scalar
+            eng.dma_start(out_2[0, 4 * q : 4 * q + 4, :].bitcast(I32), os_[32 * q : 32 * q + 4, :].bitcast(I32))

@@ -1,6 +1,7 @@
 from contextlib import ExitStack
 
 import concourse.mybir as mybir
+from concourse.masks import make_identity
 
 F32 = mybir.dt.float32
 BF16 = mybir.dt.bfloat16
@@ -31,8 +32,8 @@ def tile_picked_densedothopg_none_po_kernel(
         keep = ctx.enter_context(tc.tile_pool(name="keep", bufs=1))
         psum = ctx.enter_context(tc.psum_pool(name="psum", bufs=1))
 
-        def tile(shape, dtype, name):
-            return keep.tile(shape, dtype, name=name, align_bytes=64)
+        def tile(shape, dtype, name, tag=None):
+            return keep.tile(shape, dtype, name=name, tag=tag or name, align_bytes=64)
 
         def load_list(src, name):
             lst = tile([P, S // 16], U16, name)
@@ -46,35 +47,32 @@ def tile_picked_densedothopg_none_po_kernel(
         w1s_raw = tile([P, S], U8, "w1s_raw")
         ds_win = tile([P, T], U8, "ds_win")
         ds_mx = tile([P, S], U8, "ds_mx")
-        nc.gpsimd.memset(w1s_raw[:].bitcast(I32), 0)
         nc.vector.memset(xs_win[:].bitcast(I32), 0)
-        warm = tile([P, 2], F32, "warm")
-        nc.vector.memset(warm[:, 0:1], 0.0)
+        nc.vector.memset(w1s_raw[:].bitcast(I32), 0)
         nc.vector.memset(ds_win[:].bitcast(I32), 0)
         nc.vector.memset(ds_mx[:].bitcast(I32), 0)
 
         offs_t = load_list(offs, "offs_t")
+        k1_t = load_list(k1, "k1_t")
+        n2_t = load_list(n2, "n2_t")
+        n1_t = load_list(n1, "n1_t")
+        n3_t = load_list(n3, "n3_t")
+        n4_t = load_list(n4, "n4_t")
+        n5_t = load_list(n5, "n5_t")
         xw_win = tile([P, T], I32, "xw_win")
         nc.sync.dma_start(xw_win[:], x_words[0].rearrange("p n t -> p (n t)").bitcast(I32))
         w1w_raw = tile([P, 2 * S], U8, "w1w_raw")
-        nc.scalar.dma_start(w1w_raw[:].bitcast(I32), w1_words[0].bitcast(I32))
+        nc.gpsimd.dma_start(w1w_raw[:].bitcast(I32), w1_words[0].bitcast(I32))
         for q in range(4):
             nc.scalar.dma_start(xs_win[32 * q : 32 * q + 4, :].bitcast(I32), x_scales[0, 4 * q : 4 * q + 4, :].bitcast(I32))
         for q in range(4):
-            eng = nc.gpsimd if q < 2 else nc.scalar
+            eng = nc.gpsimd if q == 3 else nc.scalar
             eng.dma_start(w1s_raw[32 * q : 32 * q + 4, :].bitcast(I32), w1_scales[0, 4 * q : 4 * q + 4, :].bitcast(I32))
-        nc.scalar.activation(warm[:, 1:2], warm[:, 0:1], ACT.Sigmoid)
         gs_raw = tile([P, PACK], F32, "gs_raw")
         nc.gpsimd.dma_start(gs_raw[:], gs.rearrange("(p t) o -> p (t o)", t=PACK))
-        nc.gpsimd.dma_start(ds_win[0:P:8, :].bitcast(I32), d_scales[0].bitcast(I32))
-        n2_t = load_list(n2, "n2_t")
-        k1_t = load_list(k1, "k1_t")
-        n1_t = load_list(n1, "n1_t")
-        n3_t = load_list(n3, "n3_t")
-        dw_win = tile([P, T], I32, "dw_win")
-        nc.sync.dma_start(dw_win[:], d_words[0].rearrange("p n t -> p (n t)").bitcast(I32))
-        n4_t = load_list(n4, "n4_t")
-        n5_t = load_list(n5, "n5_t")
+        nc.scalar.dma_start(ds_win[0:P:8, :].bitcast(I32), d_scales[0].bitcast(I32))
+        ident = tile([P, P], F32, "ident")
+        make_identity(nc, ident[:])
 
         xs = tile([P, S], U8, "xs")
         nc.vector.tensor_copy(xs[:], xs_win[:].indirect(offs_t[:]))
@@ -86,12 +84,14 @@ def tile_picked_densedothopg_none_po_kernel(
         nc.vector.tensor_copy(w1s[:].rearrange("p (t m) -> p t m", t=PACK), w1s_raw[:].rearrange("p (m t) -> p t m", t=PACK))
         xw = tile([P, S], U32, "xw")
         nc.vector.tensor_copy(xw[:], xw_win[:].bitcast(U32).indirect(offs_t[:]))
+        dw_win = tile([P, T], I32, "dw_win", tag="xw_win")
+        nc.sync.dma_start(dw_win[:], d_words[0].rearrange("p n t -> p (n t)").bitcast(I32))
         gain = tile([P, PACK], F32, "gain")
-        nc.vector.tensor_scalar(gain[:], gs_raw[:], 0.75, None, ALU.mult)
+        nc.scalar.activation(gain[:], gs_raw[:], ACT.Copy, scale=0.75)
 
         y, yg = [], []
         for t in range(PACK):
-            acc = psum.tile([P, S], F32, name=f"y_acc{t}")
+            acc = psum.tile([P, S], F32, name=f"y_acc{t}", tag=f"bank{t}")
             nc.tensor.matmul_mx(
                 out=acc[:],
                 lhsT=w1w[:, 2 * P * t : 2 * P * (t + 1)].bitcast(FP4X4),
@@ -117,27 +117,16 @@ def tile_picked_densedothopg_none_po_kernel(
         h = [tile([P, S], F32, f"h{t}") for t in range(PACK)]
         sig0 = tile([P, S], F32, "sig0")
         dw = tile([P, S], U32, "dw")
-        for c, (c0, w) in enumerate(PIECES):
+
+        def products(name, c0, w, t, pa, pb, tag=None):
+            g2 = tile([P, w], F32, f"g2_{name}_{t}", tag=tag)
+            nc.vector.tensor_copy(g2[:], y[t][:].indirect(entries(n2_t, c0, w)))
+            nc.vector.tensor_tensor(pa[:, t, :], y[t][:].indirect(entries(n1_t, c0, w)), yg[t][:, c0 : c0 + w], ALU.mult)
+            nc.vector.tensor_tensor(pb[:, t, :], yg[t][:].indirect(entries(n3_t, c0, w)), g2[:], ALU.mult)
+
+        def second_product(c, zb):
+            c0, w = PIECES[c]
             cols = slice(c0, c0 + w)
-            g2 = tile([P, PACK, w], F32, f"g2_{c}")
-            pa = tile([P, PACK, w], F32, f"pa_{c}")
-            pb = tile([P, PACK, w], F32, f"pb_{c}")
-            for t in range(PACK):
-                nc.vector.tensor_copy(g2[:, t, :], y[t][:].indirect(entries(n2_t, c0, w)))
-                nc.vector.tensor_tensor(pa[:, t, :], y[t][:].indirect(entries(n1_t, c0, w)), yg[t][:, cols], ALU.mult)
-                nc.vector.tensor_tensor(pb[:, t, :], yg[t][:].indirect(entries(n3_t, c0, w)), g2[:, t, :], ALU.mult)
-            if c == 0:
-                dw_g = tile([P, S], U32, "dw_g")
-                nc.vector.tensor_copy(dw_g[:], dw_win[:].bitcast(U32).indirect(k1_t[:]))
-            zb = tile([P, PACK * w], BF16, f"zb_{c}")
-            nc.vector.tensor_tensor(
-                zb[:].rearrange("p (c i t) -> p c t i", i=2, t=PACK),
-                pa[:].rearrange("p t (c i) -> p c t i", i=2),
-                pb[:].rearrange("p t (c i) -> p c t i", i=2),
-                ALU.add,
-            )
-            if c == 0:
-                nc.vector.tensor_copy(dw[:].rearrange("p (t m) -> p t m", t=PACK), dw_g[:].rearrange("p (m t) -> p t m", t=PACK))
             zw = tile([P, w], U32, f"zw_{c}")
             zs = tile([P, w], U8, f"zs_{c}")
             nc.vector.quantize_mx(out=zw[:].bitcast(FP8X4), scales=zs[:], in_=zb[:])
@@ -154,6 +143,48 @@ def tile_picked_densedothopg_none_po_kernel(
             nc.scalar.activation(sig0[:, cols], h_acc[0][:, cols], ACT.Sigmoid, scale=0.0625)
             for t in range(PACK):
                 nc.scalar.activation(h[t][:, cols], h_acc[t][:, cols], ACT.Copy, scale=0.0625)
+
+        early = 3 * P
+        pa = tile([P, PACK, early], F32, "pa_early")
+        pb = tile([P, PACK, early], F32, "pb_early")
+        summed = [psum.tile([P, PACK, P], F32, name=f"summed{g}", tag=f"bank{g}") for g in range(3)]
+        zt = [tile([P, 2, P, 2], BF16, f"zt{g}") for g in range(3)]
+        for t in range(PACK):
+            products("early", 0, early, t, pa, pb)
+            for g in range(3):
+                blk = slice(P * g, P * (g + 1))
+                nc.tensor.matmul(summed[g][:, t, :], pa[:, t, blk], ident[:], start=True, stop=False, is_transpose=True)
+                nc.tensor.matmul(summed[g][:, t, :], pb[:, t, blk], ident[:], start=False, stop=True, is_transpose=True)
+                if t % 2 == 1:
+                    u = t // 2
+                    nc.scalar.copy(zt[g][:, u, :, :], summed[g][:, 2 * u : 2 * u + 2, :].rearrange("j e p -> j p e"))
+        dw_g = tile([P, S], U32, "dw_g")
+        nc.vector.tensor_copy(dw_g[:], dw_win[:].bitcast(U32).indirect(k1_t[:]))
+        nc.vector.tensor_copy(dw[:].rearrange("p (t m) -> p t m", t=PACK), dw_g[:].rearrange("p (m t) -> p t m", t=PACK))
+        zb = [tile([P, PACK * w], BF16, f"zb_{c}") for c, (c0, w) in enumerate(PIECES)]
+        for g in range(3):
+            zt_words = zt[g][:].rearrange("j u p e -> j (u p e)").bitcast(F32)
+            back = psum.tile([P, 2, P], F32, name=f"back{g}", tag=f"bank{g}")
+            for u in range(2):
+                nc.tensor.transpose(back[:, u, :], zt_words[:, P * u : P * (u + 1)], ident[:])
+            b = g % 2
+            nc.scalar.copy(
+                zb[g // 2][:, PACK * P * b : PACK * P * (b + 1)].bitcast(F32).rearrange("p (j u) -> p j u", u=2),
+                back[:].rearrange("p u j -> p j u"),
+            )
+            if g > 0:
+                second_product(g - 1, zb[g - 1])
+        pa = tile([P, PACK, P], F32, "pa_late")
+        pb = tile([P, PACK, P], F32, "pb_late")
+        for t in range(PACK):
+            products("late", early, P, t, pa, pb, tag={2: "zb_0", 3: "zb_1"}.get(t))
+        nc.vector.tensor_tensor(
+            zb[2][:].rearrange("p (c i t) -> p c t i", i=2, t=PACK),
+            pa[:].rearrange("p t (c i) -> p c t i", i=2),
+            pb[:].rearrange("p t (c i) -> p c t i", i=2),
+            ALU.add,
+        )
+        second_product(2, zb[2])
 
         st = [tile([P, S], F32, f"st{t}") for t in range(PACK)]
         nst = [tile([P, S], F32, f"nst{t}") for t in range(PACK)]

@@ -30,10 +30,14 @@ def tile_picked_densedothopg_none_po_kernel(
     nc = tc.nc
     with ExitStack() as ctx:
         keep = ctx.enter_context(tc.tile_pool(name="keep", bufs=1))
+        turn = ctx.enter_context(tc.tile_pool(name="turn", bufs=1))
         psum = ctx.enter_context(tc.psum_pool(name="psum", bufs=1))
 
         def tile(shape, dtype, name, tag=None):
             return keep.tile(shape, dtype, name=name, tag=tag or name, align_bytes=64)
+
+        def placed(shape, dtype, name, offset):
+            return turn.tile(shape, dtype, name=name, align_bytes=64, offset=offset)
 
         def load_list(src, name):
             lst = tile([P, S // 16], U16, name)
@@ -69,8 +73,9 @@ def tile_picked_densedothopg_none_po_kernel(
             eng = nc.gpsimd if q == 3 else nc.scalar
             eng.dma_start(w1s_raw[32 * q : 32 * q + 4, :].bitcast(I32), w1_scales[0, 4 * q : 4 * q + 4, :].bitcast(I32))
         gs_raw = tile([P, PACK], F32, "gs_raw")
-        nc.gpsimd.dma_start(gs_raw[:], gs.rearrange("(p t) o -> p (t o)", t=PACK))
-        nc.scalar.dma_start(ds_win[0:P:8, :].bitcast(I32), d_scales[0].bitcast(I32))
+        nc.vector.memset(gs_raw[:], 0.0)
+        nc.scalar.dma_start(gs_raw[:], gs.rearrange("(p t) o -> p (t o)", t=PACK))
+        nc.gpsimd.dma_start(ds_win[0:P:8, :].bitcast(I32), d_scales[0].bitcast(I32))
         ident = tile([P, P], F32, "ident")
         make_identity(nc, ident[:])
 
@@ -87,6 +92,8 @@ def tile_picked_densedothopg_none_po_kernel(
         dw_win = tile([P, T], I32, "dw_win", tag="xw_win")
         nc.sync.dma_start(dw_win[:], d_words[0].rearrange("p n t -> p (n t)").bitcast(I32))
         gain = tile([P, PACK], F32, "gain")
+        warm = tile([P, 1], F32, "warm")
+        nc.scalar.activation(warm[:], gs_raw[:, 0:1], ACT.Sigmoid)
         nc.scalar.activation(gain[:], gs_raw[:], ACT.Copy, scale=0.75)
 
         y, yg = [], []
@@ -118,8 +125,7 @@ def tile_picked_densedothopg_none_po_kernel(
         sig0 = tile([P, S], F32, "sig0")
         dw = tile([P, S], U32, "dw")
 
-        def products(name, c0, w, t, pa, pb, tag=None):
-            g2 = tile([P, w], F32, f"g2_{name}_{t}", tag=tag)
+        def products(g2, c0, w, t, pa, pb):
             nc.vector.tensor_copy(g2[:], y[t][:].indirect(entries(n2_t, c0, w)))
             nc.vector.tensor_tensor(pa[:, t, :], y[t][:].indirect(entries(n1_t, c0, w)), yg[t][:, c0 : c0 + w], ALU.mult)
             nc.vector.tensor_tensor(pb[:, t, :], yg[t][:].indirect(entries(n3_t, c0, w)), g2[:], ALU.mult)
@@ -150,7 +156,8 @@ def tile_picked_densedothopg_none_po_kernel(
         summed = [psum.tile([P, PACK, P], F32, name=f"summed{g}", tag=f"bank{g}") for g in range(3)]
         zt = [tile([P, 2, P, 2], BF16, f"zt{g}") for g in range(3)]
         for t in range(PACK):
-            products("early", 0, early, t, pa, pb)
+            g2 = tile([P, early], F32, f"g2_early{t}") if t < 3 else placed([P, early], F32, "g2_early3", 1984)
+            products(g2, 0, early, t, pa, pb)
             for g in range(3):
                 blk = slice(P * g, P * (g + 1))
                 nc.tensor.matmul(summed[g][:, t, :], pa[:, t, blk], ident[:], start=True, stop=False, is_transpose=True)
@@ -158,7 +165,7 @@ def tile_picked_densedothopg_none_po_kernel(
                 if t % 2 == 1:
                     u = t // 2
                     nc.scalar.copy(zt[g][:, u, :, :], summed[g][:, 2 * u : 2 * u + 2, :].rearrange("j e p -> j p e"))
-        dw_g = tile([P, S], U32, "dw_g")
+        dw_g = placed([P, S], U32, "dw_g", 0)
         nc.vector.tensor_copy(dw_g[:], dw_win[:].bitcast(U32).indirect(k1_t[:]))
         nc.vector.tensor_copy(dw[:].rearrange("p (t m) -> p t m", t=PACK), dw_g[:].rearrange("p (m t) -> p t m", t=PACK))
         zb = [tile([P, PACK * w], BF16, f"zb_{c}") for c, (c0, w) in enumerate(PIECES)]
@@ -174,10 +181,11 @@ def tile_picked_densedothopg_none_po_kernel(
             )
             if g > 0:
                 second_product(g - 1, zb[g - 1])
-        pa = tile([P, PACK, P], F32, "pa_late")
+        pa = placed([P, PACK, P], F32, "pa_late", 3072)
         pb = tile([P, PACK, P], F32, "pb_late")
         for t in range(PACK):
-            products("late", early, P, t, pa, pb, tag={2: "zb_0", 3: "zb_1"}.get(t))
+            g2 = placed([P, P], F32, f"g2_late{t}", 2048 + 512 * t) if t < 2 else tile([P, P], F32, f"g2_late{t}", tag=f"zb_{t - 2}")
+            products(g2, early, P, t, pa, pb)
         nc.vector.tensor_tensor(
             zb[2][:].rearrange("p (c i t) -> p c t i", i=2, t=PACK),
             pa[:].rearrange("p t (c i) -> p c t i", i=2),

@@ -147,7 +147,7 @@ def tile_picked_densedothopg_none_po_kernel(
                     stop=True,
                 )
             nc.scalar.activation(sig0[:, cols], h_acc[0][:, cols], ACT.Sigmoid, scale=0.0625)
-            for t in range(PACK):
+            for t in range(PACK if c < 2 else 1):
                 nc.scalar.activation(h[t][:, cols], h_acc[t][:, cols], ACT.Copy, scale=0.0625)
 
         early = 3 * P
@@ -167,6 +167,9 @@ def tile_picked_densedothopg_none_po_kernel(
                     nc.scalar.copy(zt[g][:, u, :, :], summed[g][:, 2 * u : 2 * u + 2, :].rearrange("j e p -> j p e"))
         dw_g = placed([P, S], U32, "dw_g", 0)
         nc.vector.tensor_copy(dw_g[:], dw_win[:].bitcast(U32).indirect(k1_t[:]))
+        pa_late = placed([P, PACK, P], F32, "pa_late", 3072)
+        pb_late = tile([P, PACK, P], F32, "pb_late")
+        products(placed([P, P], F32, "g2_late0", 2048), early, P, 0, pa_late, pb_late)
         nc.vector.tensor_copy(dw[:].rearrange("p (t m) -> p t m", t=PACK), dw_g[:].rearrange("p (m t) -> p t m", t=PACK))
         zb = [tile([P, PACK * w], BF16, f"zb_{c}") for c, (c0, w) in enumerate(PIECES)]
         for g in range(3):
@@ -181,9 +184,8 @@ def tile_picked_densedothopg_none_po_kernel(
             )
             if g > 0:
                 second_product(g - 1, zb[g - 1])
-        pa = placed([P, PACK, P], F32, "pa_late", 3072)
-        pb = tile([P, PACK, P], F32, "pb_late")
-        for t in range(PACK):
+        pa, pb = pa_late, pb_late
+        for t in range(1, PACK):
             g2 = placed([P, P], F32, f"g2_late{t}", 2048 + 512 * t) if t < 2 else tile([P, P], F32, f"g2_late{t}", tag=f"zb_{t - 2}")
             products(g2, early, P, t, pa, pb)
         nc.vector.tensor_tensor(
@@ -196,11 +198,15 @@ def tile_picked_densedothopg_none_po_kernel(
 
         st = [tile([P, S], F32, f"st{t}") for t in range(PACK)]
         nst = [tile([P, S], F32, f"nst{t}") for t in range(PACK)]
-        res = [tile([P, PACK, w], F32, f"res_{c}") for c, (c0, w) in enumerate(PIECES)]
+        res = [tile([P, PACK, PIECES[0][1]], F32, "res_0")]
+
+        out_rows = out_0.rearrange("(p t) s -> p t s", t=PACK)
 
         def difference(c, t):
             c0, w = PIECES[c]
             nc.vector.tensor_tensor(res[c][:, t, :], nst[t][:].indirect(entries(n5_t, c0, w)), st[t][:, c0 : c0 + w], ALU.add)
+            if c == 0:
+                nc.sync.dma_start(out_rows[:, t, c0 : c0 + w], res[c][:, t, :])
 
         for t in range(PACK):
             if t == 0:
@@ -210,6 +216,7 @@ def tile_picked_densedothopg_none_po_kernel(
                     )
             else:
                 sg = tile([P, S], F32, f"sg{t}")
+                nc.scalar.activation(h[t][:, early:], h_acc[t][:, early:], ACT.Copy, scale=0.0625)
                 for c0, w in HALVES:
                     nc.scalar.activation(sg[:, c0 : c0 + w], h[t][:].indirect(entries(n4_t, c0, w)), ACT.Sigmoid)
                 nc.vector.tensor_tensor(st[t][:], sg[:], h[t][:], ALU.mult)
@@ -221,25 +228,34 @@ def tile_picked_densedothopg_none_po_kernel(
                 difference(0, t - 1)
         difference(0, PACK - 1)
 
-        out_rows = out_0.rearrange("(p t) s -> p t s", t=PACK)
+        res.append(tile([P, PACK, P], F32, "res_1", tag="sg3"))
+        res.append(tile([P, PACK, P], F32, "res_2", tag="h3"))
         out_words = out_1[0].rearrange("p n t -> p (n t)").bitcast(I32)
         os_ = tile([P, S], U8, "os")
-        for c, (c0, w) in enumerate(PIECES):
-            cols = slice(c0, c0 + w)
-            if c > 0:
-                for t in range(PACK):
-                    difference(c, t)
-            nc.sync.dma_start(out_rows[:, :, cols], res[c][:])
-            ob = tile([P, PACK * w], BF16, f"ob_{c}")
-            dst = ob[:].rearrange("p (c i t) -> p c t i", i=2, t=PACK)
-            srcv = res[c][:].rearrange("p t (c i) -> p c t i", i=2)
-            if c < len(PIECES) - 1:
-                nc.scalar.copy(dst, srcv)
-            else:
-                nc.vector.tensor_copy(dst, srcv)
-            ow = tile([P, w], U32, f"ow_{c}")
-            nc.vector.quantize_mx(out=ow[:].bitcast(FP8X4), scales=os_[:, cols], in_=ob[:])
-            nc.scalar.dma_start(out_words[:, cols], ow[:].bitcast(I32))
+        ow = tile([P, S], U32, "ow")
+        ob = [tile([P, PACK * w], BF16, f"ob_{c}") for c, (c0, w) in enumerate(PIECES)]
+
+        def rounded(c, copy):
+            copy(ob[c][:].rearrange("p (c i t) -> p c t i", i=2, t=PACK), res[c][:].rearrange("p t (c i) -> p c t i", i=2))
+
+        def planes(c):
+            c0, w = PIECES[c]
+            nc.vector.quantize_mx(out=ow[:, c0 : c0 + w].bitcast(FP8X4), scales=os_[:, c0 : c0 + w], in_=ob[c][:])
+
+        rounded(0, nc.scalar.copy)
+        for c in (1, 2):
+            c0, w = PIECES[c]
+            for t in range(PACK):
+                difference(c, t)
+            nc.sync.dma_start(out_rows[:, :, c0 : c0 + w], res[c][:])
+            if c == 1:
+                rounded(1, nc.scalar.copy)
+        planes(0)
+        nc.scalar.dma_start(out_words[:, 0:256], ow[:, 0:256].bitcast(I32))
+        rounded(2, nc.vector.tensor_copy)
+        planes(1)
+        planes(2)
+        nc.scalar.dma_start(out_words[:, 256:S], ow[:, 256:S].bitcast(I32))
         for q in range(4):
-            eng = nc.sync if q % 2 == 0 else nc.scalar
+            eng = nc.sync if q < 3 else nc.scalar
             eng.dma_start(out_2[0, 4 * q : 4 * q + 4, :].bitcast(I32), os_[32 * q : 32 * q + 4, :].bitcast(I32))

from contextlib import ExitStack

import concourse.mybir as mybir
from concourse.masks import make_identity

F32 = mybir.dt.float32
BF16 = mybir.dt.bfloat16
I32 = mybir.dt.int32
U32 = mybir.dt.uint32
U16 = mybir.dt.uint16
U8 = mybir.dt.uint8
FP8X4 = mybir.dt.float8_e4m3fn_x4
FP4X4 = mybir.dt.float4_e2m1fn_x4
ALU = mybir.AluOpType
ACT = mybir.ActivationFunctionType

P = 128
PACK = 4
S = 512
T = 2048
PIECES = ((0, 256), (256, 128), (384, 128))
HALVES = ((0, 256), (256, 256))

FLOPS = 2 * 2 * 512 * 512 * 512


def tile_picked_densedothopg_none_po_kernel(
    tc, x_words, x_scales, w1_words, w1_scales, gs, d_words, d_scales, offs, n1, n2, n3, k1, n4, n5, out_0, out_1, out_2
):
    nc = tc.nc
    with ExitStack() as ctx:
        keep = ctx.enter_context(tc.tile_pool(name="keep", bufs=1))
        turn = ctx.enter_context(tc.tile_pool(name="turn", bufs=1))
        psum = ctx.enter_context(tc.psum_pool(name="psum", bufs=1))

        def tile(shape, dtype, name, tag=None):
            return keep.tile(shape, dtype, name=name, tag=tag or name, align_bytes=64)

        def placed(shape, dtype, name, offset):
            return turn.tile(shape, dtype, name=name, align_bytes=64, offset=offset)

        def load_list(src, name):
            lst = tile([P, S // 16], U16, name)
            nc.sync.dma_start(lst[:], src)
            return lst

        def entries(lst, c0, w):
            return lst[:, c0 // 16 : (c0 + w) // 16]

        xs_win = tile([P, T], U8, "xs_win")
        w1s_raw = tile([P, S], U8, "w1s_raw")
        ds_win = tile([P, T], U8, "ds_win")
        ds_mx = tile([P, S], U8, "ds_mx")
        nc.vector.memset(xs_win[:].bitcast(I32), 0)
        nc.vector.memset(w1s_raw[:].bitcast(I32), 0)
        nc.vector.memset(ds_win[:].bitcast(I32), 0)
        nc.vector.memset(ds_mx[:].bitcast(I32), 0)

        offs_t = load_list(offs, "offs_t")
        k1_t = load_list(k1, "k1_t")
        n2_t = load_list(n2, "n2_t")
        n1_t = load_list(n1, "n1_t")
        n3_t = load_list(n3, "n3_t")
        n4_t = load_list(n4, "n4_t")
        n5_t = load_list(n5, "n5_t")
        xw_win = tile([P, T], I32, "xw_win")
        nc.sync.dma_start(xw_win[:], x_words[0].rearrange("p n t -> p (n t)").bitcast(I32))
        w1w_raw = tile([P, 2 * S], U8, "w1w_raw")
        nc.gpsimd.dma_start(w1w_raw[:].bitcast(I32), w1_words[0].bitcast(I32))
        for q in range(4):
            nc.scalar.dma_start(xs_win[32 * q : 32 * q + 4, :].bitcast(I32), x_scales[0, 4 * q : 4 * q + 4, :].bitcast(I32))
        for q in range(4):
            eng = nc.gpsimd if q == 3 else nc.scalar
            eng.dma_start(w1s_raw[32 * q : 32 * q + 4, :].bitcast(I32), w1_scales[0, 4 * q : 4 * q + 4, :].bitcast(I32))
        gs_raw = tile([P, PACK], F32, "gs_raw")
        nc.vector.memset(gs_raw[:], 0.0)
        nc.scalar.dma_start(gs_raw[:], gs.rearrange("(p t) o -> p (t o)", t=PACK))
        nc.gpsimd.dma_start(ds_win[0:P:8, :].bitcast(I32), d_scales[0].bitcast(I32))
        ident = tile([P, P], F32, "ident")
        make_identity(nc, ident[:])

        xs = tile([P, S], U8, "xs")
        nc.vector.tensor_copy(xs[:], xs_win[:].indirect(offs_t[:]))
        w1w = tile([P, 2 * S], U8, "w1w")
        nc.vector.tensor_copy(
            w1w[:].rearrange("p (t m b) -> p t m b", t=PACK, b=2), w1w_raw[:].rearrange("p (m t b) -> p t m b", t=PACK, b=2)
        )
        w1s = tile([P, S], U8, "w1s")
        nc.vector.tensor_copy(w1s[:].rearrange("p (t m) -> p t m", t=PACK), w1s_raw[:].rearrange("p (m t) -> p t m", t=PACK))
        xw = tile([P, S], U32, "xw")
        nc.vector.tensor_copy(xw[:], xw_win[:].bitcast(U32).indirect(offs_t[:]))
        dw_win = tile([P, T], I32, "dw_win", tag="xw_win")
        nc.sync.dma_start(dw_win[:], d_words[0].rearrange("p n t -> p (n t)").bitcast(I32))
        gain = tile([P, PACK], F32, "gain")
        warm = tile([P, 1], F32, "warm")
        nc.scalar.activation(warm[:], gs_raw[:, 0:1], ACT.Sigmoid)
        nc.scalar.activation(gain[:], gs_raw[:], ACT.Copy, scale=0.75)

        y, yg = [], []
        for t in range(PACK):
            acc = psum.tile([P, S], F32, name=f"y_acc{t}", tag=f"bank{t}")
            nc.tensor.matmul_mx(
                out=acc[:],
                lhsT=w1w[:, 2 * P * t : 2 * P * (t + 1)].bitcast(FP4X4),
                lhsT_scale=w1s[:, P * t : P * (t + 1)],
                rhs=xw[:].bitcast(FP8X4),
                rhs_scale=xs[:],
                start=True,
                stop=True,
            )
            y.append(tile([P, S], F32, f"y{t}"))
            yg.append(tile([P, S], F32, f"yg{t}"))
            nc.scalar.copy(y[t][:], acc[:])
            nc.scalar.activation(yg[t][:], acc[:], ACT.Copy, scale=gain[:, t : t + 1])

        ds_g = tile([P, S], U8, "ds_g")
        nc.vector.tensor_copy(ds_g[:], ds_win[:].indirect(k1_t[:]))
        ds_d = tile([P, S], U8, "ds_d")
        nc.vector.tensor_copy(ds_d[:].rearrange("p (t m) -> p t m", t=PACK), ds_g[:].rearrange("p (m t) -> p t m", t=PACK))
        for r in range(4):
            nc.sync.dma_start(ds_mx[r:P:32, :].bitcast(I32), ds_d[8 * r : P : 32, :].bitcast(I32))

        h_acc = [psum.tile([P, S], F32, name=f"h_acc{t}") for t in range(PACK)]
        h = [tile([P, S], F32, f"h{t}") for t in range(PACK)]
        sig0 = tile([P, S], F32, "sig0")
        dw = tile([P, S], U32, "dw")

        def products(g2, c0, w, t, pa, pb):
            nc.vector.tensor_copy(g2[:], y[t][:].indirect(entries(n2_t, c0, w)))
            nc.vector.tensor_tensor(pa[:, t, :], y[t][:].indirect(entries(n1_t, c0, w)), yg[t][:, c0 : c0 + w], ALU.mult)
            nc.vector.tensor_tensor(pb[:, t, :], yg[t][:].indirect(entries(n3_t, c0, w)), g2[:], ALU.mult)

        def second_product(c, zb):
            c0, w = PIECES[c]
            cols = slice(c0, c0 + w)
            zw = tile([P, w], U32, f"zw_{c}")
            zs = tile([P, w], U8, f"zs_{c}")
            nc.vector.quantize_mx(out=zw[:].bitcast(FP8X4), scales=zs[:], in_=zb[:])
            for t in range(PACK):
                nc.tensor.matmul_mx(
                    out=h_acc[t][:, cols],
                    lhsT=dw[:, P * t : P * (t + 1)].bitcast(FP8X4),
                    lhsT_scale=ds_mx[:, P * t : P * (t + 1)],
                    rhs=zw[:].bitcast(FP8X4),
                    rhs_scale=zs[:],
                    start=True,
                    stop=True,
                )
            nc.scalar.activation(sig0[:, cols], h_acc[0][:, cols], ACT.Sigmoid, scale=0.0625)
            for t in range(PACK if c < 2 else 1):
                nc.scalar.activation(h[t][:, cols], h_acc[t][:, cols], ACT.Copy, scale=0.0625)

        early = 3 * P
        pa = tile([P, PACK, early], F32, "pa_early")
        pb = tile([P, PACK, early], F32, "pb_early")
        summed = [psum.tile([P, PACK, P], F32, name=f"summed{g}", tag=f"bank{g}") for g in range(3)]
        zt = [tile([P, 2, P, 2], BF16, f"zt{g}") for g in range(3)]
        for t in range(PACK):
            g2 = tile([P, early], F32, f"g2_early{t}") if t < 3 else placed([P, early], F32, "g2_early3", 1984)
            products(g2, 0, early, t, pa, pb)
            for g in range(3):
                blk = slice(P * g, P * (g + 1))
                nc.tensor.matmul(summed[g][:, t, :], pa[:, t, blk], ident[:], start=True, stop=False, is_transpose=True)
                nc.tensor.matmul(summed[g][:, t, :], pb[:, t, blk], ident[:], start=False, stop=True, is_transpose=True)
                if t % 2 == 1:
                    u = t // 2
                    nc.scalar.copy(zt[g][:, u, :, :], summed[g][:, 2 * u : 2 * u + 2, :].rearrange("j e p -> j p e"))
        dw_g = placed([P, S], U32, "dw_g", 0)
        nc.vector.tensor_copy(dw_g[:], dw_win[:].bitcast(U32).indirect(k1_t[:]))
        pa_late = placed([P, PACK, P], F32, "pa_late", 3072)
        pb_late = tile([P, PACK, P], F32, "pb_late")
        products(placed([P, P], F32, "g2_late0", 2048), early, P, 0, pa_late, pb_late)
        nc.vector.tensor_copy(dw[:].rearrange("p (t m) -> p t m", t=PACK), dw_g[:].rearrange("p (m t) -> p t m", t=PACK))
        zb = [tile([P, PACK * w], BF16, f"zb_{c}") for c, (c0, w) in enumerate(PIECES)]
        for g in range(3):
            zt_words = zt[g][:].rearrange("j u p e -> j (u p e)").bitcast(F32)
            back = psum.tile([P, 2, P], F32, name=f"back{g}", tag=f"bank{g}")
            for u in range(2):
                nc.tensor.transpose(back[:, u, :], zt_words[:, P * u : P * (u + 1)], ident[:])
            b = g % 2
            nc.scalar.copy(
                zb[g // 2][:, PACK * P * b : PACK * P * (b + 1)].bitcast(F32).rearrange("p (j u) -> p j u", u=2),
                back[:].rearrange("p u j -> p j u"),
            )
            if g > 0:
                second_product(g - 1, zb[g - 1])
        pa, pb = pa_late, pb_late
        for t in range(1, PACK):
            g2 = placed([P, P], F32, f"g2_late{t}", 2048 + 512 * t) if t < 2 else tile([P, P], F32, f"g2_late{t}", tag=f"zb_{t - 2}")
            products(g2, early, P, t, pa, pb)
        nc.vector.tensor_tensor(
            zb[2][:].rearrange("p (c i t) -> p c t i", i=2, t=PACK),
            pa[:].rearrange("p t (c i) -> p c t i", i=2),
            pb[:].rearrange("p t (c i) -> p c t i", i=2),
            ALU.add,
        )
        second_product(2, zb[2])

        st = [tile([P, S], F32, f"st{t}") for t in range(PACK)]
        nst = [tile([P, S], F32, f"nst{t}") for t in range(PACK)]
        res = [tile([P, PACK, PIECES[0][1]], F32, "res_0")]

        out_rows = out_0.rearrange("(p t) s -> p t s", t=PACK)

        def difference(c, t):
            c0, w = PIECES[c]
            nc.vector.tensor_tensor(res[c][:, t, :], nst[t][:].indirect(entries(n5_t, c0, w)), st[t][:, c0 : c0 + w], ALU.add)
            if c == 0:
                nc.sync.dma_start(out_rows[:, t, c0 : c0 + w], res[c][:, t, :])

        for t in range(PACK):
            if t == 0:
                for c0, w in HALVES:
                    nc.vector.tensor_tensor(
                        st[0][:, c0 : c0 + w], sig0[:].indirect(entries(n4_t, c0, w)), h[0][:, c0 : c0 + w], ALU.mult
                    )
            else:
                sg = tile([P, S], F32, f"sg{t}")
                nc.scalar.activation(h[t][:, early:], h_acc[t][:, early:], ACT.Copy, scale=0.0625)
                for c0, w in HALVES:
                    nc.scalar.activation(sg[:, c0 : c0 + w], h[t][:].indirect(entries(n4_t, c0, w)), ACT.Sigmoid)
                nc.vector.tensor_tensor(st[t][:], sg[:], h[t][:], ALU.mult)
            if t < 2:
                nc.vector.tensor_scalar(nst[t][:], st[t][:], -1.0, None, ALU.mult)
            else:
                nc.scalar.activation(nst[t][:], st[t][:], ACT.Copy, scale=-1.0)
            if t > 0:
                difference(0, t - 1)
        difference(0, PACK - 1)

        res.append(tile([P, PACK, P], F32, "res_1", tag="sg3"))
        res.append(tile([P, PACK, P], F32, "res_2", tag="h3"))
        out_words = out_1[0].rearrange("p n t -> p (n t)").bitcast(I32)
        os_ = tile([P, S], U8, "os")
        ow = tile([P, S], U32, "ow")
        ob = [tile([P, PACK * w], BF16, f"ob_{c}") for c, (c0, w) in enumerate(PIECES)]

        def rounded(c, copy):
            copy(ob[c][:].rearrange("p (c i t) -> p c t i", i=2, t=PACK), res[c][:].rearrange("p t (c i) -> p c t i", i=2))

        def planes(c):
            c0, w = PIECES[c]
            nc.vector.quantize_mx(out=ow[:, c0 : c0 + w].bitcast(FP8X4), scales=os_[:, c0 : c0 + w], in_=ob[c][:])

        rounded(0, nc.scalar.copy)
        for c in (1, 2):
            c0, w = PIECES[c]
            for t in range(PACK):
                difference(c, t)
            nc.sync.dma_start(out_rows[:, :, c0 : c0 + w], res[c][:])
            if c == 1:
                rounded(1, nc.scalar.copy)
        planes(0)
        nc.scalar.dma_start(out_words[:, 0:256], ow[:, 0:256].bitcast(I32))
        rounded(2, nc.vector.tensor_copy)
        planes(1)
        planes(2)
        nc.scalar.dma_start(out_words[:, 256:S], ow[:, 256:S].bitcast(I32))
        for q in range(4):
            eng = nc.sync if q < 3 else nc.scalar
            eng.dma_start(out_2[0, 4 * q : 4 * q + 4, :].bitcast(I32), os_[32 * q : 32 * q + 4, :].bitcast(I32))
